import numpy as np
import ml_dtypes


def mxq(x, axis, fmt="e4m3"):
    dtype, down = {"e4m3": (ml_dtypes.float8_e4m3fn, 7), "e5m2": (ml_dtypes.float8_e5m2, 14)}[fmt]
    v = np.moveaxis(np.asarray(x, np.float32).astype(ml_dtypes.bfloat16).astype(np.float64), axis, -1)
    blocks = v.reshape(v.shape[:-1] + (-1, 32))
    amax = np.abs(blocks).max(-1, keepdims=True)
    byte = np.maximum(np.where(amax > 0, np.frexp(amax)[1] - 1 + 127, 0) - down, 1)
    scale = np.exp2(byte - 127.0)
    codes = (blocks / scale).astype(np.float32).astype(dtype).astype(np.float64)
    return np.moveaxis((codes * scale).reshape(v.shape), -1, axis)


WIDE = False


def mx_kscale(k):
    if not WIDE:
        return np.ones(k)
    levels = np.array([30, -30])
    if k % 512:
        return np.exp2(np.random.permutation(np.resize(levels, k // 32))).repeat(32)
    a = np.empty((k // 512, 16))
    for p in range(k // 512):
        a[p, :8] = np.random.permutation(np.resize(levels, 8))
        for g in range(8):
            far = levels[np.abs(levels - a[p, g]) >= 10]
            a[p, g + 8] = far[np.random.randint(len(far))]
    return np.exp2(a.ravel()).repeat(32)


def f64(x):
    return np.asarray(x).astype(np.float64)


def striped(idx):
    return np.tile(np.asarray(idx).reshape(-1, 16).T, (8, 1)).astype(np.uint16)


def unstriped(offs):
    return offs[:16].T.reshape(-1).astype(np.int64)


E2M1 = np.array([0.0, 0.5, 1.0, 1.5, 2.0, 3.0, 4.0, 6.0, -0.0, -0.5, -1.0, -1.5, -2.0, -3.0, -4.0, -6.0])


def pack_weight(w, fmt):
    k, n = w.shape
    w = f64(np.asarray(w, np.float32).astype(ml_dtypes.bfloat16)).reshape(k // 32, 32, n)
    amax = np.abs(w).max(1)
    if fmt in ("e4m3", "e5m2"):
        byte = np.frexp(amax)[1] - 1 + 127 - (7 if fmt == "e4m3" else 14)
    else:
        mant, ex = np.frexp(amax / 6.0)
        byte = np.where(mant > 0.5, ex, ex - 1) + 127
    byte = np.clip(np.where(amax > 0, byte, 1), 1, 254)
    scaled = (w * np.exp2(127.0 - byte)[:, None, :]).reshape(k, n).astype(np.float32)
    by_word = np.ascontiguousarray(scaled.reshape(k // 512, 128, 4, n).transpose(0, 1, 3, 2))
    if fmt in ("e4m3", "e5m2"):
        words = by_word.astype(ml_dtypes.float8_e4m3fn if fmt == "e4m3" else ml_dtypes.float8_e5m2).view(np.uint8)
    else:
        c = by_word.astype(ml_dtypes.float4_e2m1fn).view(np.uint8) & 0xF
        words = (c[..., 0::2] | (c[..., 1::2] << 4)).reshape(k // 512, 128, 2 * n)
    return np.ascontiguousarray(words), np.ascontiguousarray(byte.astype(np.uint8).reshape(k // 512, 16, n))


def unpack_weight(words, scales, fmt):
    g, _, n = scales.shape
    words = np.ascontiguousarray(words).reshape(g, 128, n, -1)
    if fmt in ("e4m3", "e5m2"):
        vals = words.view(ml_dtypes.float8_e4m3fn if fmt == "e4m3" else ml_dtypes.float8_e5m2).astype(np.float64)
    else:
        nib = np.empty((g, 128, n, 4), np.uint8)
        nib[..., 0::2] = words & 0xF
        nib[..., 1::2] = words >> 4
        vals = E2M1[nib]
    vals = vals * np.repeat(np.exp2(scales.astype(np.float64) - 127.0), 8, axis=1)[..., None]
    return vals.transpose(0, 1, 3, 2).reshape(g * 512, n)


def sigmoid(v):
    return 1.0 / (1.0 + np.exp(-v))


K, T, J, R, O, N, E = 512, 2048, 256, 512, 128, 256, 1024


def setup_inputs():
    n = np.random.standard_normal
    idx = np.random.permutation(T)[:J]
    idx2 = np.random.permutation(T)[:J]
    idx3 = np.random.permutation(J)[:O]
    idx4 = np.random.permutation(J)[:O]
    idx5 = np.random.permutation(E)[:O]
    fk = mx_kscale(K)
    fr = mx_kscale(R)
    xtp = pack_weight(n((K, T)) / fk[:, None], "e2m1")
    wp = pack_weight(n((K, R)) * 1 / np.sqrt(K) * fk[:, None], "e4m3")
    w2p = pack_weight(n((K, R)) * 1 / np.sqrt(K) * fk[:, None] * fr, "e5m2")
    wbp = pack_weight(n((R, N)) * 1 / np.sqrt(R) / fr[:, None], "e2m1")
    return {
        "xt_words": xtp[0],
        "xt_scales": xtp[1],
        "w_words": wp[0],
        "w_scales": wp[1],
        "w2_words": w2p[0],
        "w2_scales": w2p[1],
        "sg": (np.random.uniform(0.6, 1.6, (R, 1))).astype(np.float32),
        "bg": (np.random.uniform(-1.0, 1.0, (R, 1))).astype(np.float32),
        "wb_words": wbp[0],
        "wb_scales": wbp[1],
        "tz": (n((N, E))).astype(np.float32),
        "offs": striped(idx),
        "offs2": striped(idx2),
        "offs3": striped(idx3),
        "offs4": striped(idx4),
        "offs5": striped(idx5),
    }


def reference(xt_words, xt_scales, w_words, w_scales, w2_words, w2_scales, sg, bg, wb_words, wb_scales, tz, offs, offs2, offs3, offs4, offs5):
    idx = unstriped(offs)
    idx2 = unstriped(offs2)
    idx3 = unstriped(offs3)
    idx4 = unstriped(offs4)
    idx5 = unstriped(offs5)
    xtu = unpack_weight(xt_words, xt_scales, "e2m1")
    wu = unpack_weight(w_words, w_scales, "e4m3")
    w2u = unpack_weight(w2_words, w2_scales, "e5m2")
    wbu = unpack_weight(wb_words, wb_scales, "e2m1")
    xtidxg = xtu[:, idx]
    a = wu.T @ xtidxg
    xtidx2g = xtu[:, idx2]
    b = w2u.T @ xtidx2g
    hid = b[:, idx4] * sigmoid(a[:, idx3] * f64(sg) + f64(bg))
    hidq = mxq(hid, 0, "e5m2")
    p = wbu.T @ hidq
    y = p + f64(tz)[:, idx5]
    return y

@@ -1,0 +1,153 @@
+from contextlib import ExitStack
+
+import concourse.mybir as mybir
+
+K, T, J, R, O, N, E = 512, 2048, 256, 512, 128, 256, 1024
+FLOPS = 2 * K * R * J * 2 + 2 * R * N * O
+
+F32 = mybir.dt.float32
+BF16 = mybir.dt.bfloat16
+I32 = mybir.dt.int32
+U32 = mybir.dt.uint32
+U16 = mybir.dt.uint16
+U8 = mybir.dt.uint8
+E4M3X4 = mybir.dt.float8_e4m3fn_x4
+E5M2X4 = mybir.dt.float8_e5m2_x4
+E2M1X4 = mybir.dt.float4_e2m1fn_x4
+ACT = mybir.ActivationFunctionType
+ALU = mybir.AluOpType
+
+P = 128
+PACK = 4
+QUAD = 32
+
+
+def load_scale_rows(queue, plane, scales, r):
+    queue.dma_start(out=plane[r:P:QUAD, :].bitcast(I32), in_=scales[0].bitcast(I32)[r : 16 : PACK, :])
+
+
+def tile_list_ahead_gatefetch_one_tabled_kernel(
+    tc, xt_words, xt_scales, w_words, w_scales, w2_words, w2_scales, sg, bg, wb_words, wb_scales, tz,
+    offs, offs2, offs3, offs4, offs5, out,
+):
+    nc = tc.nc
+    with ExitStack() as ctx:
+        lists = ctx.enter_context(tc.tile_pool(name="lists", bufs=1))
+        sb = ctx.enter_context(tc.tile_pool(name="sb", bufs=1))
+        psum = ctx.enter_context(tc.psum_pool(name="psum", bufs=1))
+
+        l1 = lists.tile([P, J // 16], U16, name="l1")
+        l2 = lists.tile([P, J // 16], U16, name="l2")
+        l3 = lists.tile([P, O // 16], U16, name="l3")
+        l4 = lists.tile([P, O // 16], U16, name="l4")
+        l5 = lists.tile([P, O // 16], U16, name="l5")
+
+        xw = sb.tile([P, T], U16, name="xw", align_bytes=64)
+        xs = sb.tile([P, T], U8, name="xs", align_bytes=64)
+        w_raw = sb.tile([P, R], I32, name="w_raw", align_bytes=64)
+        w2_raw = sb.tile([P, R], I32, name="w2_raw", align_bytes=64)
+        ws_raw = sb.tile([P, R], U8, name="ws_raw", tag="ws_raw", align_bytes=64)
+        w2s_raw = sb.tile([P, R], U8, name="w2s_raw", align_bytes=64)
+        wbw = sb.tile([P, 2 * N], U8, name="wbw", align_bytes=64)
+        wbs = sb.tile([P, N], U8, name="wbs", align_bytes=64)
+        slope = sb.tile([P, PACK], F32, name="slope")
+        shift = sb.tile([P, PACK], F32, name="shift")
+
+        nc.gpsimd.memset(ws_raw[:].bitcast(I32), 0)
+        for plane in (xs, w2s_raw, wbs):
+            nc.vector.memset(plane[:].bitcast(I32), 0)
+
+        warm_in = sb.tile([P, 1], F32, name="warm_in")
+        warm_out = sb.tile([P, 1], F32, name="warm_out")
+        nc.vector.memset(warm_in[:], 0.0)
+        nc.scalar.activation(out=warm_out[:], in_=warm_in[:], func=ACT.Sigmoid)
+
+        tables = [sb.tile([P, E], F32, name=f"table{h}") for h in range(N // P)]
+        nc.sync.dma_start(l1[:], offs)
+        nc.sync.dma_start(l2[:], offs2)
+        nc.sync.dma_start(l3[:], offs3)
+        nc.sync.dma_start(out=xw[:].bitcast(I32), in_=xt_words[0].bitcast(I32))
+        for r in range(PACK):
+            load_scale_rows(nc.sync, xs, xt_scales, r)
+        nc.sync.dma_start(out=w_raw[:], in_=w_words[0].rearrange("p c b -> p (c b)").bitcast(I32))
+        for r in range(PACK):
+            load_scale_rows(nc.sync if r < 2 else nc.gpsimd, ws_raw, w_scales, r)
+        nc.sync.dma_start(out=w2_raw[:], in_=w2_words[0].rearrange("p c b -> p (c b)").bitcast(I32))
+        for r in range(PACK):
+            load_scale_rows(nc.sync, w2s_raw, w2_scales, r)
+        nc.sync.dma_start(out=slope[:], in_=sg.rearrange("(p t) one -> p (t one)", t=PACK))
+        nc.sync.dma_start(out=shift[:], in_=bg.rearrange("(p t) one -> p (t one)", t=PACK))
+        nc.sync.dma_start(l4[:], offs4)
+        nc.sync.dma_start(l5[:], offs5)
+        nc.sync.dma_start(out=wbw[:].bitcast(I32), in_=wb_words[0].bitcast(I32))
+        nc.sync.dma_start(out=tables[0][:], in_=tz[0:P, :])
+        for r in range(PACK):
+            load_scale_rows(nc.gpsimd if r < 2 else nc.sync, wbs, wb_scales, r)
+        nc.sync.dma_start(out=tables[1][:], in_=tz[P : 2 * P, :])
+
+        x1s = sb.tile([P, J], U8, name="x1s", align_bytes=64)
+        x1w = sb.tile([P, J], U16, name="x1w", align_bytes=64)
+        x2s = sb.tile([P, J], U8, name="x2s", align_bytes=64)
+        x2w = sb.tile([P, J], U16, name="x2w", tag="ws_raw", align_bytes=64)
+        wp = sb.tile([P, R], U32, name="wp", align_bytes=64)
+        w2p = sb.tile([P, R], U32, name="w2p", align_bytes=64)
+        wsp = sb.tile([P, R], U8, name="wsp", align_bytes=64)
+        w2sp = sb.tile([P, R], U8, name="w2sp", align_bytes=64)
+
+        def deal(copy, dst, src):
+            copy(out=dst.rearrange("p (t m) -> p m t", t=PACK), in_=src.rearrange("p (m t) -> p m t", t=PACK))
+
+        nc.vector.tensor_copy(x1w[:], xw[:].indirect(l1[:]))
+        nc.vector.tensor_copy(x1s[:], xs[:].indirect(l1[:]))
+        deal(nc.scalar.copy, wp[:], w_raw[:].bitcast(U32))
+        deal(nc.vector.tensor_copy, wsp[:], ws_raw[:])
+        nc.vector.tensor_copy(x2s[:], xs[:].indirect(l2[:]))
+        nc.vector.tensor_copy(x2w[:], xw[:].indirect(l2[:]))
+        deal(nc.scalar.copy, w2p[:], w2_raw[:].bitcast(U32))
+        deal(nc.vector.tensor_copy, w2sp[:], w2s_raw[:])
+
+        gate = sb.tile([P, PACK, O], F32, name="gate")
+        picked = sb.tile([P, PACK, O], F32, name="picked")
+        for t in range(PACK):
+            cols = slice(P * t, P * (t + 1))
+            acc = psum.tile([P, J], F32, name=f"acc_a{t}", tag=f"bank{t}")
+            nc.tensor.matmul_mx(out=acc[:], lhsT=wp[:, cols].bitcast(E4M3X4), lhsT_scale=wsp[:, cols],
+                                rhs=x1w[:].bitcast(E2M1X4), rhs_scale=x1s[:], start=True, stop=True)
+            a_rows = sb.tile([P, J], F32, name=f"a_rows{t}", tag=f"a_rows{t}")
+            (nc.scalar.copy if t < PACK - 1 else nc.vector.tensor_copy)(out=a_rows[:], in_=acc[:])
+            nc.scalar.activation(out=gate[:, t, :], in_=a_rows[:].indirect(l3[:]), func=ACT.Sigmoid,
+                                 bias=shift[:, t : t + 1], scale=slope[:, t : t + 1])
+        for t in range(PACK):
+            cols = slice(P * t, P * (t + 1))
+            acc = psum.tile([P, J], F32, name=f"acc_b{t}", tag=f"bank{PACK + t}")
+            nc.tensor.matmul_mx(out=acc[:], lhsT=w2p[:, cols].bitcast(E5M2X4), lhsT_scale=w2sp[:, cols],
+                                rhs=x2w[:].bitcast(E2M1X4), rhs_scale=x2s[:], start=True, stop=True)
+            b_rows = sb.tile([P, J], F32, name=f"b_rows{t}", tag=f"b_rows{t}")
+            if t < PACK - 1:
+                nc.vector.tensor_copy(out=b_rows[:], in_=acc[:])
+                nc.vector.tensor_copy(picked[:, t, :], b_rows[:].indirect(l4[:]))
+            else:
+                nc.scalar.copy(out=b_rows[:], in_=acc[:])
+                nc.scalar.activation(out=picked[:, t, :], in_=b_rows[:].indirect(l4[:]), func=ACT.Copy)
+
+        hid = sb.tile([P, O * PACK], BF16, name="hid", align_bytes=64)
+        nc.vector.tensor_tensor(
+            out=hid[:].rearrange("p (c i t) -> p c t i", i=4, t=PACK),
+            in0=picked[:].rearrange("p t (c i) -> p c t i", i=4),
+            in1=gate[:].rearrange("p t (c i) -> p c t i", i=4),
+            op=ALU.mult,
+        )
+        hw = sb.tile([P, O], U32, name="hw", align_bytes=64)
+        hs = sb.tile([P, O], U8, name="hs", align_bytes=64)
+        nc.vector.quantize_mx(out=hw[:].bitcast(E5M2X4), scales=hs[:], in_=hid[:])
+
+        for h in range(N // P):
+            entries = sb.tile([P, O], F32, name=f"entries{h}", tag=("a_rows3", "b_rows3")[h])
+            nc.scalar.activation(out=entries[:], in_=tables[h][:].indirect(l5[:]), func=ACT.Copy)
+            acc = psum.tile([P, O], F32, name=f"acc_p{h}", tag=f"bank{h}")
+            nc.tensor.matmul_mx(out=acc[:], lhsT=wbw[:, 2 * P * h : 2 * P * (h + 1)].bitcast(E2M1X4),
+                                lhsT_scale=wbs[:, P * h : P * (h + 1)], rhs=hw[:].bitcast(E5M2X4), rhs_scale=hs[:],
+                                start=True, stop=True)
+            result = sb.tile([P, O], F32, name=f"result{h}")
+            nc.vector.tensor_tensor(out=result[:], in0=acc[:], in1=entries[:], op=ALU.add)
+            (nc.sync if h == 0 else nc.scalar).dma_start(out=out[P * h : P * (h + 1), :], in_=result[:])

@@ -20,6 +20,7 @@ ALU = mybir.AluOpType
 P = 128
 PACK = 4
 QUAD = 32
+XS_SPLIT = 1664
 
 
 def load_scale_rows(queue, plane, scales, r):
@@ -53,8 +54,9 @@ def tile_list_ahead_gatefetch_one_tabled_kernel(
         slope = sb.tile([P, PACK], F32, name="slope")
         shift = sb.tile([P, PACK], F32, name="shift")
 
-        nc.gpsimd.memset(ws_raw[:].bitcast(I32), 0)
-        for plane in (xs, w2s_raw, wbs):
+        nc.gpsimd.memset(xs[:, XS_SPLIT:].bitcast(I32), 0)
+        nc.vector.memset(xs[:, :XS_SPLIT].bitcast(I32), 0)
+        for plane in (ws_raw, w2s_raw, wbs):
             nc.vector.memset(plane[:].bitcast(I32), 0)
 
         warm_in = sb.tile([P, 1], F32, name="warm_in")
@@ -65,16 +67,16 @@ def tile_list_ahead_gatefetch_one_tabled_kernel(
         tables = [sb.tile([P, E], F32, name=f"table{h}") for h in range(N // P)]
         nc.sync.dma_start(l1[:], offs)
         nc.sync.dma_start(l2[:], offs2)
-        nc.sync.dma_start(l3[:], offs3)
-        nc.sync.dma_start(out=xw[:].bitcast(I32), in_=xt_words[0].bitcast(I32))
-        for r in range(PACK):
-            load_scale_rows(nc.sync, xs, xt_scales, r)
         nc.sync.dma_start(out=w_raw[:], in_=w_words[0].rearrange("p c b -> p (c b)").bitcast(I32))
         for r in range(PACK):
-            load_scale_rows(nc.sync if r < 2 else nc.gpsimd, ws_raw, w_scales, r)
+            load_scale_rows(nc.sync, xs, xt_scales, r)
+        nc.sync.dma_start(out=xw[:].bitcast(I32), in_=xt_words[0].bitcast(I32))
+        for r in range(PACK):
+            load_scale_rows(nc.sync, ws_raw, w_scales, r)
         nc.sync.dma_start(out=w2_raw[:], in_=w2_words[0].rearrange("p c b -> p (c b)").bitcast(I32))
         for r in range(PACK):
-            load_scale_rows(nc.sync, w2s_raw, w2_scales, r)
+            load_scale_rows(nc.sync if r < 2 else nc.gpsimd, w2s_raw, w2_scales, r)
+        nc.sync.dma_start(l3[:], offs3)
         nc.sync.dma_start(out=slope[:], in_=sg.rearrange("(p t) one -> p (t one)", t=PACK))
         nc.sync.dma_start(out=shift[:], in_=bg.rearrange("(p t) one -> p (t one)", t=PACK))
         nc.sync.dma_start(l4[:], offs4)
@@ -97,14 +99,16 @@ def tile_list_ahead_gatefetch_one_tabled_kernel(
         def deal(copy, dst, src):
             copy(out=dst.rearrange("p (t m) -> p m t", t=PACK), in_=src.rearrange("p (m t) -> p m t", t=PACK))
 
-        nc.vector.tensor_copy(x1w[:], xw[:].indirect(l1[:]))
         nc.vector.tensor_copy(x1s[:], xs[:].indirect(l1[:]))
+        nc.vector.tensor_copy(x1w[:], xw[:].indirect(l1[:]))
         deal(nc.scalar.copy, wp[:], w_raw[:].bitcast(U32))
-        deal(nc.vector.tensor_copy, wsp[:], ws_raw[:])
+        for t in range(PACK):
+            nc.vector.tensor_copy(out=wsp[:, P * t : P * (t + 1)], in_=ws_raw[:, t:R:PACK])
         nc.vector.tensor_copy(x2s[:], xs[:].indirect(l2[:]))
         nc.vector.tensor_copy(x2w[:], xw[:].indirect(l2[:]))
         deal(nc.scalar.copy, w2p[:], w2_raw[:].bitcast(U32))
-        deal(nc.vector.tensor_copy, w2sp[:], w2s_raw[:])
+        for t in range(PACK):
+            nc.vector.tensor_copy(out=w2sp[:, P * t : P * (t + 1)], in_=w2s_raw[:, t:R:PACK])
 
         gate = sb.tile([P, PACK, O], F32, name="gate")
         picked = sb.tile([P, PACK, O], F32, name="picked")
@@ -114,7 +118,7 @@ def tile_list_ahead_gatefetch_one_tabled_kernel(
             nc.tensor.matmul_mx(out=acc[:], lhsT=wp[:, cols].bitcast(E4M3X4), lhsT_scale=wsp[:, cols],
                                 rhs=x1w[:].bitcast(E2M1X4), rhs_scale=x1s[:], start=True, stop=True)
             a_rows = sb.tile([P, J], F32, name=f"a_rows{t}", tag=f"a_rows{t}")
-            (nc.scalar.copy if t < PACK - 1 else nc.vector.tensor_copy)(out=a_rows[:], in_=acc[:])
+            (nc.scalar.copy if t < 2 else nc.vector.tensor_copy)(out=a_rows[:], in_=acc[:])
             nc.scalar.activation(out=gate[:, t, :], in_=a_rows[:].indirect(l3[:]), func=ACT.Sigmoid,
                                  bias=shift[:, t : t + 1], scale=slope[:, t : t + 1])
         for t in range(PACK):
@@ -122,13 +126,12 @@ def tile_list_ahead_gatefetch_one_tabled_kernel(
             acc = psum.tile([P, J], F32, name=f"acc_b{t}", tag=f"bank{PACK + t}")
             nc.tensor.matmul_mx(out=acc[:], lhsT=w2p[:, cols].bitcast(E5M2X4), lhsT_scale=w2sp[:, cols],
                                 rhs=x2w[:].bitcast(E2M1X4), rhs_scale=x2s[:], start=True, stop=True)
-            b_rows = sb.tile([P, J], F32, name=f"b_rows{t}", tag=f"b_rows{t}")
+            b_rows = sb.tile([P, J], F32, name=f"b_rows{t}", tag=f"b_rows{t}" if t < 2 else f"a_rows{5 - t}")[:]
+            (nc.vector.tensor_copy if t < 2 else nc.scalar.copy)(out=b_rows, in_=acc[:])
             if t < PACK - 1:
-                nc.vector.tensor_copy(out=b_rows[:], in_=acc[:])
-                nc.vector.tensor_copy(picked[:, t, :], b_rows[:].indirect(l4[:]))
+                nc.vector.tensor_copy(picked[:, t, :], b_rows.indirect(l4[:]))
             else:
-                nc.scalar.copy(out=b_rows[:], in_=acc[:])
-                nc.scalar.activation(out=picked[:, t, :], in_=b_rows[:].indirect(l4[:]), func=ACT.Copy)
+                nc.scalar.activation(out=picked[:, t, :], in_=b_rows.indirect(l4[:]), func=ACT.Copy)
 
         hid = sb.tile([P, O * PACK], BF16, name="hid", align_bytes=64)
         nc.vector.tensor_tensor(
@@ -141,13 +144,13 @@ def tile_list_ahead_gatefetch_one_tabled_kernel(
         hs = sb.tile([P, O], U8, name="hs", align_bytes=64)
         nc.vector.quantize_mx(out=hw[:].bitcast(E5M2X4), scales=hs[:], in_=hid[:])
 
+        entries = sb.tile([P, N // P, O], F32, name="entries", tag="a_rows2")
         for h in range(N // P):
-            entries = sb.tile([P, O], F32, name=f"entries{h}", tag=("a_rows3", "b_rows3")[h])
-            nc.scalar.activation(out=entries[:], in_=tables[h][:].indirect(l5[:]), func=ACT.Copy)
+            nc.scalar.activation(out=entries[:, h, :], in_=tables[h][:].indirect(l5[:]), func=ACT.Copy)
             acc = psum.tile([P, O], F32, name=f"acc_p{h}", tag=f"bank{h}")
             nc.tensor.matmul_mx(out=acc[:], lhsT=wbw[:, 2 * P * h : 2 * P * (h + 1)].bitcast(E2M1X4),
                                 lhsT_scale=wbs[:, P * h : P * (h + 1)], rhs=hw[:].bitcast(E5M2X4), rhs_scale=hs[:],
                                 start=True, stop=True)
             result = sb.tile([P, O], F32, name=f"result{h}")
-            nc.vector.tensor_tensor(out=result[:], in0=acc[:], in1=entries[:], op=ALU.add)
+            nc.vector.tensor_tensor(out=result[:], in0=acc[:], in1=entries[:, h, :], op=ALU.add)
             (nc.sync if h == 0 else nc.scalar).dma_start(out=out[P * h : P * (h + 1), :], in_=result[:])

@@ -35,6 +35,7 @@ def tile_list_ahead_gatefetch_one_tabled_kernel(
     with ExitStack() as ctx:
         lists = ctx.enter_context(tc.tile_pool(name="lists", bufs=1))
         sb = ctx.enter_context(tc.tile_pool(name="sb", bufs=1))
+        late = ctx.enter_context(tc.tile_pool(name="late", bufs=1))
         psum = ctx.enter_context(tc.psum_pool(name="psum", bufs=1))
 
         l1 = lists.tile([P, J // 16], U16, name="l1")
@@ -83,9 +84,9 @@ def tile_list_ahead_gatefetch_one_tabled_kernel(
         nc.sync.dma_start(l5[:], offs5)
         nc.sync.dma_start(out=wbw[:].bitcast(I32), in_=wb_words[0].bitcast(I32))
         nc.sync.dma_start(out=tables[0][:], in_=tz[0:P, :])
-        for r in range(PACK):
-            load_scale_rows(nc.gpsimd if r < 2 else nc.sync, wbs, wb_scales, r)
         nc.sync.dma_start(out=tables[1][:], in_=tz[P : 2 * P, :])
+        for r in range(PACK):
+            load_scale_rows(nc.sync, wbs, wb_scales, r)
 
         x1s = sb.tile([P, J], U8, name="x1s", align_bytes=64)
         x1w = sb.tile([P, J], U16, name="x1w", align_bytes=64)
@@ -117,8 +118,11 @@ def tile_list_ahead_gatefetch_one_tabled_kernel(
             acc = psum.tile([P, J], F32, name=f"acc_a{t}", tag=f"bank{t}")
             nc.tensor.matmul_mx(out=acc[:], lhsT=wp[:, cols].bitcast(E4M3X4), lhsT_scale=wsp[:, cols],
                                 rhs=x1w[:].bitcast(E2M1X4), rhs_scale=x1s[:], start=True, stop=True)
-            a_rows = sb.tile([P, J], F32, name=f"a_rows{t}", tag=f"a_rows{t}")
-            (nc.scalar.copy if t < 2 else nc.vector.tensor_copy)(out=a_rows[:], in_=acc[:])
+            if t < PACK - 1:
+                a_rows = sb.tile([P, J], F32, name=f"a_rows{t}")
+            else:
+                a_rows = late.tile([P, J], F32, name=f"a_rows{t}", offset=2 * J)
+            (nc.scalar.copy if t == 0 else nc.vector.tensor_copy)(out=a_rows[:], in_=acc[:])
             nc.scalar.activation(out=gate[:, t, :], in_=a_rows[:].indirect(l3[:]), func=ACT.Sigmoid,
                                  bias=shift[:, t : t + 1], scale=slope[:, t : t + 1])
         for t in range(PACK):
@@ -126,7 +130,10 @@ def tile_list_ahead_gatefetch_one_tabled_kernel(
             acc = psum.tile([P, J], F32, name=f"acc_b{t}", tag=f"bank{PACK + t}")
             nc.tensor.matmul_mx(out=acc[:], lhsT=w2p[:, cols].bitcast(E5M2X4), lhsT_scale=w2sp[:, cols],
                                 rhs=x2w[:].bitcast(E2M1X4), rhs_scale=x2s[:], start=True, stop=True)
-            b_rows = sb.tile([P, J], F32, name=f"b_rows{t}", tag=f"b_rows{t}" if t < 2 else f"a_rows{5 - t}")[:]
+            if t < 2:
+                b_rows = sb.tile([P, J], F32, name=f"b_rows{t}")[:]
+            else:
+                b_rows = late.tile([P, J], F32, name=f"b_rows{t}", offset=4 * J * (t - 2))[:]
             (nc.vector.tensor_copy if t < 2 else nc.scalar.copy)(out=b_rows, in_=acc[:])
             if t < PACK - 1:
                 nc.vector.tensor_copy(picked[:, t, :], b_rows.indirect(l4[:]))
@@ -134,17 +141,18 @@ def tile_list_ahead_gatefetch_one_tabled_kernel(
                 nc.scalar.activation(out=picked[:, t, :], in_=b_rows.indirect(l4[:]), func=ACT.Copy)
 
         hid = sb.tile([P, O * PACK], BF16, name="hid", align_bytes=64)
+        hw = sb.tile([P, O], U32, name="hw", align_bytes=64)
+        hs = sb.tile([P, O], U8, name="hs", align_bytes=64)
+
         nc.vector.tensor_tensor(
             out=hid[:].rearrange("p (c i t) -> p c t i", i=4, t=PACK),
             in0=picked[:].rearrange("p t (c i) -> p c t i", i=4),
             in1=gate[:].rearrange("p t (c i) -> p c t i", i=4),
             op=ALU.mult,
         )
-        hw = sb.tile([P, O], U32, name="hw", align_bytes=64)
-        hs = sb.tile([P, O], U8, name="hs", align_bytes=64)
         nc.vector.quantize_mx(out=hw[:].bitcast(E5M2X4), scales=hs[:], in_=hid[:])
 
-        entries = sb.tile([P, N // P, O], F32, name="entries", tag="a_rows2")
+        entries = late.tile([P, N // P, O], F32, name="entries", offset=4 * J)
         for h in range(N // P):
             nc.scalar.activation(out=entries[:, h, :], in_=tables[h][:].indirect(l5[:]), func=ACT.Copy)
             acc = psum.tile([P, O], F32, name=f"acc_p{h}", tag=f"bank{h}")

@@ -109,7 +109,7 @@ def tile_list_ahead_gatefetch_one_tabled_kernel(
         nc.vector.tensor_copy(x2w[:], xw[:].indirect(l2[:]))
         deal(nc.scalar.copy, w2p[:], w2_raw[:].bitcast(U32))
         for t in range(PACK):
-            nc.vector.tensor_copy(out=w2sp[:, P * t : P * (t + 1)], in_=w2s_raw[:, t:R:PACK])
+            nc.gpsimd.tensor_copy(out=w2sp[:, P * t : P * (t + 1)], in_=w2s_raw[:, t:R:PACK])
 
         gate = sb.tile([P, PACK, O], F32, name="gate")
         picked = sb.tile([P, PACK, O], F32, name="picked")

from contextlib import ExitStack

import concourse.mybir as mybir

K, T, J, R, O, N, E = 512, 2048, 256, 512, 128, 256, 1024
FLOPS = 2 * K * R * J * 2 + 2 * R * N * O

F32 = mybir.dt.float32
BF16 = mybir.dt.bfloat16
I32 = mybir.dt.int32
U32 = mybir.dt.uint32
U16 = mybir.dt.uint16
U8 = mybir.dt.uint8
E4M3X4 = mybir.dt.float8_e4m3fn_x4
E5M2X4 = mybir.dt.float8_e5m2_x4
E2M1X4 = mybir.dt.float4_e2m1fn_x4
ACT = mybir.ActivationFunctionType
ALU = mybir.AluOpType

P = 128
PACK = 4
QUAD = 32
XS_SPLIT = 1664


def load_scale_rows(queue, plane, scales, r):
    queue.dma_start(out=plane[r:P:QUAD, :].bitcast(I32), in_=scales[0].bitcast(I32)[r : 16 : PACK, :])


def tile_list_ahead_gatefetch_one_tabled_kernel(
    tc, xt_words, xt_scales, w_words, w_scales, w2_words, w2_scales, sg, bg, wb_words, wb_scales, tz,
    offs, offs2, offs3, offs4, offs5, out,
):
    nc = tc.nc
    with ExitStack() as ctx:
        lists = ctx.enter_context(tc.tile_pool(name="lists", bufs=1))
        sb = ctx.enter_context(tc.tile_pool(name="sb", bufs=1))
        late = ctx.enter_context(tc.tile_pool(name="late", bufs=1))
        psum = ctx.enter_context(tc.psum_pool(name="psum", bufs=1))

        l1 = lists.tile([P, J // 16], U16, name="l1")
        l2 = lists.tile([P, J // 16], U16, name="l2")
        l3 = lists.tile([P, O // 16], U16, name="l3")
        l4 = lists.tile([P, O // 16], U16, name="l4")
        l5 = lists.tile([P, O // 16], U16, name="l5")

        xw = sb.tile([P, T], U16, name="xw", align_bytes=64)
        xs = sb.tile([P, T], U8, name="xs", align_bytes=64)
        w_raw = sb.tile([P, R], I32, name="w_raw", align_bytes=64)
        w2_raw = sb.tile([P, R], I32, name="w2_raw", align_bytes=64)
        ws_raw = sb.tile([P, R], U8, name="ws_raw", tag="ws_raw", align_bytes=64)
        w2s_raw = sb.tile([P, R], U8, name="w2s_raw", align_bytes=64)
        wbw = sb.tile([P, 2 * N], U8, name="wbw", align_bytes=64)
        wbs = sb.tile([P, N], U8, name="wbs", align_bytes=64)
        slope = sb.tile([P, PACK], F32, name="slope")
        shift = sb.tile([P, PACK], F32, name="shift")

        nc.gpsimd.memset(xs[:, XS_SPLIT:].bitcast(I32), 0)
        nc.vector.memset(xs[:, :XS_SPLIT].bitcast(I32), 0)
        for plane in (ws_raw, w2s_raw, wbs):
            nc.vector.memset(plane[:].bitcast(I32), 0)

        warm_in = sb.tile([P, 1], F32, name="warm_in")
        warm_out = sb.tile([P, 1], F32, name="warm_out")
        nc.vector.memset(warm_in[:], 0.0)
        nc.scalar.activation(out=warm_out[:], in_=warm_in[:], func=ACT.Sigmoid)

        tables = [sb.tile([P, E], F32, name=f"table{h}") for h in range(N // P)]
        nc.sync.dma_start(l1[:], offs)
        nc.sync.dma_start(l2[:], offs2)
        nc.sync.dma_start(out=w_raw[:], in_=w_words[0].rearrange("p c b -> p (c b)").bitcast(I32))
        for r in range(PACK):
            load_scale_rows(nc.sync, xs, xt_scales, r)
        nc.sync.dma_start(out=xw[:].bitcast(I32), in_=xt_words[0].bitcast(I32))
        for r in range(PACK):
            load_scale_rows(nc.sync, ws_raw, w_scales, r)
        nc.sync.dma_start(out=w2_raw[:], in_=w2_words[0].rearrange("p c b -> p (c b)").bitcast(I32))
        for r in range(PACK):
            load_scale_rows(nc.sync if r < 2 else nc.gpsimd, w2s_raw, w2_scales, r)
        nc.sync.dma_start(l3[:], offs3)
        nc.sync.dma_start(out=slope[:], in_=sg.rearrange("(p t) one -> p (t one)", t=PACK))
        nc.sync.dma_start(out=shift[:], in_=bg.rearrange("(p t) one -> p (t one)", t=PACK))
        nc.sync.dma_start(l4[:], offs4)
        nc.sync.dma_start(l5[:], offs5)
        nc.sync.dma_start(out=wbw[:].bitcast(I32), in_=wb_words[0].bitcast(I32))
        nc.sync.dma_start(out=tables[0][:], in_=tz[0:P, :])
        nc.sync.dma_start(out=tables[1][:], in_=tz[P : 2 * P, :])
        for r in range(PACK):
            load_scale_rows(nc.sync, wbs, wb_scales, r)

        x1s = sb.tile([P, J], U8, name="x1s", align_bytes=64)
        x1w = sb.tile([P, J], U16, name="x1w", align_bytes=64)
        x2s = sb.tile([P, J], U8, name="x2s", align_bytes=64)
        x2w = sb.tile([P, J], U16, name="x2w", tag="ws_raw", align_bytes=64)
        wp = sb.tile([P, R], U32, name="wp", align_bytes=64)
        w2p = sb.tile([P, R], U32, name="w2p", align_bytes=64)
        wsp = sb.tile([P, R], U8, name="wsp", align_bytes=64)
        w2sp = sb.tile([P, R], U8, name="w2sp", align_bytes=64)

        def deal(copy, dst, src):
            copy(out=dst.rearrange("p (t m) -> p m t", t=PACK), in_=src.rearrange("p (m t) -> p m t", t=PACK))

        nc.vector.tensor_copy(x1s[:], xs[:].indirect(l1[:]))
        nc.vector.tensor_copy(x1w[:], xw[:].indirect(l1[:]))
        deal(nc.scalar.copy, wp[:], w_raw[:].bitcast(U32))
        for t in range(PACK):
            nc.vector.tensor_copy(out=wsp[:, P * t : P * (t + 1)], in_=ws_raw[:, t:R:PACK])
        nc.vector.tensor_copy(x2s[:], xs[:].indirect(l2[:]))
        nc.vector.tensor_copy(x2w[:], xw[:].indirect(l2[:]))
        deal(nc.scalar.copy, w2p[:], w2_raw[:].bitcast(U32))
        for t in range(PACK):
            nc.gpsimd.tensor_copy(out=w2sp[:, P * t : P * (t + 1)], in_=w2s_raw[:, t:R:PACK])

        gate = sb.tile([P, PACK, O], F32, name="gate")
        picked = sb.tile([P, PACK, O], F32, name="picked")
        for t in range(PACK):
            cols = slice(P * t, P * (t + 1))
            acc = psum.tile([P, J], F32, name=f"acc_a{t}", tag=f"bank{t}")
            nc.tensor.matmul_mx(out=acc[:], lhsT=wp[:, cols].bitcast(E4M3X4), lhsT_scale=wsp[:, cols],
                                rhs=x1w[:].bitcast(E2M1X4), rhs_scale=x1s[:], start=True, stop=True)
            if t < PACK - 1:
                a_rows = sb.tile([P, J], F32, name=f"a_rows{t}")
            else:
                a_rows = late.tile([P, J], F32, name=f"a_rows{t}", offset=2 * J)
            (nc.scalar.copy if t == 0 else nc.vector.tensor_copy)(out=a_rows[:], in_=acc[:])
            nc.scalar.activation(out=gate[:, t, :], in_=a_rows[:].indirect(l3[:]), func=ACT.Sigmoid,
                                 bias=shift[:, t : t + 1], scale=slope[:, t : t + 1])
        for t in range(PACK):
            cols = slice(P * t, P * (t + 1))
            acc = psum.tile([P, J], F32, name=f"acc_b{t}", tag=f"bank{PACK + t}")
            nc.tensor.matmul_mx(out=acc[:], lhsT=w2p[:, cols].bitcast(E5M2X4), lhsT_scale=w2sp[:, cols],
                                rhs=x2w[:].bitcast(E2M1X4), rhs_scale=x2s[:], start=True, stop=True)
            if t < 2:
                b_rows = sb.tile([P, J], F32, name=f"b_rows{t}")[:]
            else:
                b_rows = late.tile([P, J], F32, name=f"b_rows{t}", offset=4 * J * (t - 2))[:]
            (nc.vector.tensor_copy if t < 2 else nc.scalar.copy)(out=b_rows, in_=acc[:])
            if t < PACK - 1:
                nc.vector.tensor_copy(picked[:, t, :], b_rows.indirect(l4[:]))
            else:
                nc.scalar.activation(out=picked[:, t, :], in_=b_rows.indirect(l4[:]), func=ACT.Copy)

        hid = sb.tile([P, O * PACK], BF16, name="hid", align_bytes=64)
        hw = sb.tile([P, O], U32, name="hw", align_bytes=64)
        hs = sb.tile([P, O], U8, name="hs", align_bytes=64)

        nc.vector.tensor_tensor(
            out=hid[:].rearrange("p (c i t) -> p c t i", i=4, t=PACK),
            in0=picked[:].rearrange("p t (c i) -> p c t i", i=4),
            in1=gate[:].rearrange("p t (c i) -> p c t i", i=4),
            op=ALU.mult,
        )
        nc.vector.quantize_mx(out=hw[:].bitcast(E5M2X4), scales=hs[:], in_=hid[:])

        entries = late.tile([P, N // P, O], F32, name="entries", offset=4 * J)
        for h in range(N // P):
            nc.scalar.activation(out=entries[:, h, :], in_=tables[h][:].indirect(l5[:]), func=ACT.Copy)
            acc = psum.tile([P, O], F32, name=f"acc_p{h}", tag=f"bank{h}")
            nc.tensor.matmul_mx(out=acc[:], lhsT=wbw[:, 2 * P * h : 2 * P * (h + 1)].bitcast(E2M1X4),
                                lhsT_scale=wbs[:, P * h : P * (h + 1)], rhs=hw[:].bitcast(E5M2X4), rhs_scale=hs[:],
                                start=True, stop=True)
            result = sb.tile([P, O], F32, name=f"result{h}")
            nc.vector.tensor_tensor(out=result[:], in0=acc[:], in1=entries[:, h, :], op=ALU.add)
            (nc.sync if h == 0 else nc.scalar).dma_start(out=out[P * h : P * (h + 1), :], in_=result[:])
